import numpy as np
import ml_dtypes


def mxq(x, axis, fmt="e4m3"):
    dtype, down = {"e4m3": (ml_dtypes.float8_e4m3fn, 7), "e5m2": (ml_dtypes.float8_e5m2, 14)}[fmt]
    v = np.moveaxis(np.asarray(x, np.float32).astype(ml_dtypes.bfloat16).astype(np.float64), axis, -1)
    blocks = v.reshape(v.shape[:-1] + (-1, 32))
    amax = np.abs(blocks).max(-1, keepdims=True)
    byte = np.maximum(np.where(amax > 0, np.frexp(amax)[1] - 1 + 127, 0) - down, 1)
    scale = np.exp2(byte - 127.0)
    codes = (blocks / scale).astype(np.float32).astype(dtype).astype(np.float64)
    return np.moveaxis((codes * scale).reshape(v.shape), -1, axis)


WIDE = False


def mx_kscale(k, group=512):
    if not WIDE:
        return np.ones(k)
    levels = np.array([18, -18])
    if group != 512:
        return np.exp2(np.random.permutation(np.resize(levels, k // group))).repeat(group)
    if k % 512:
        return np.exp2(np.random.permutation(np.resize(levels, k // 32))).repeat(32)
    a = np.empty((k // 512, 16))
    for p in range(k // 512):
        a[p, :8] = np.random.permutation(np.resize(levels, 8))
        for g in range(8):
            far = levels[np.abs(levels - a[p, g]) >= 10]
            a[p, g + 8] = far[np.random.randint(len(far))]
    return np.exp2(a.ravel()).repeat(32)


def f64(x):
    return np.asarray(x).astype(np.float64)


H, D, N = 4, 128, 1024


def setup_inputs():
    n = np.random.standard_normal
    s = mx_kscale(D, 0)[:, None]
    S = n((H, D, 128)) / np.sqrt(D)
    return {
        "q": n((H, D, N)).astype(np.float32),
        "qa": (np.random.uniform(0.5, 2.0, (D, 1)) * s).astype(np.float32),
        "S": (S / s).astype(np.float32),
        "og": n((H, N, 128)).astype(np.float32),
    }


def reference(q, qa, S, og):
    fq = (1.0 / (1.0 + np.exp(-f64(q)))) * f64(qa)
    y = mxq(fq, 1, "e4m3").transpose(0, 2, 1) @ mxq(f64(S), 1, "e4m3")
    y = y / (1.0 + np.exp(-f64(og)))
    return y

@@ -1,0 +1,152 @@
+from contextlib import ExitStack
+
+import concourse.mybir as mybir
+
+H, D, N, E = 4, 128, 1024, 128
+FLOPS = 2 * H * N * D * E
+
+F32 = mybir.dt.float32
+BF16 = mybir.dt.bfloat16
+U32 = mybir.dt.uint32
+U8 = mybir.dt.uint8
+FP8X4 = mybir.dt.float8_e4m3fn_x4
+SIGMOID = mybir.ActivationFunctionType.Sigmoid
+MULT = mybir.AluOpType.mult
+
+P = 128
+ROWS = 32
+PACK = 4
+CHUNK = 512
+DEAL = CHUNK // P
+PIECE = 256
+PIECE_M = PIECE // DEAL
+
+
+def tile_rows_read_sig_gate_kernel(tc, q, qa, S, og, out):
+    nc = tc.nc
+    q_rows = q.rearrange("h (p j) n -> (h p) j n", j=PACK)
+    s_rows = S.rearrange("h (p j) e -> (h p) j e", j=PACK)
+    og_rows = og.rearrange("h (c m r) e -> c m h (r e)", m=P, r=DEAL)
+    out_rows = out.rearrange("h (c m r) e -> c m h (r e)", m=P, r=DEAL)
+
+    with ExitStack() as ctx:
+        sb = ctx.enter_context(tc.tile_pool(name="sb", bufs=1))
+        ps = ctx.enter_context(tc.psum_pool(name="ps", bufs=1))
+        ctx.enter_context(tc.manual_schedule())
+
+        q_raw = [sb.tile([P, PACK, PIECE], F32, name="q_raw%d" % i) for i in range(4)]
+        q_sig = [sb.tile([P, PIECE_M, 2, DEAL, 2], F32, name="q_sig%d" % i) for i in range(4)]
+        fq = [[sb.tile([P, 2, P, PACK], BF16, name="fq%d_%d" % (c, u), align_bytes=64) for u in range(2)] for c in range(2)]
+        fq_codes = [[sb.tile([P, 2 * P], U32, name="fqc%d_%d" % (c, u), align_bytes=64) for u in range(2)] for c in range(2)]
+        fq_scales = [[sb.tile([P, 2 * P], U8, name="fqs%d_%d" % (c, u), align_bytes=64) for u in range(2)] for c in range(2)]
+        og_raw = [[sb.tile([P, 2, CHUNK], F32, name="og_raw%d_%d" % (c, g)) for g in range(2)] for c in range(2)]
+        gate = [[sb.tile([P, CHUNK], F32, name="gate%d_%d" % (c, h)) for h in range(H)] for c in range(2)]
+        res = [[sb.tile([P, CHUNK], F32, name="res%d_%d" % (c, h)) for h in range(H)] for c in range(2)]
+        acc = [[ps.tile([P, CHUNK], F32, name="acc%d_%d" % (c, h)) for h in range(H)] for c in range(2)]
+        qa_sb = sb.tile([P, PACK], F32, name="qa_sb")
+        qa_rep = sb.tile([P, PIECE_M, PACK], F32, name="qa_rep")
+        s_raw = sb.tile([P, PACK, E], F32, name="s_raw")
+        s_bf = sb.tile([P, E, PACK], BF16, name="s_bf", align_bytes=64)
+        s_codes = sb.tile([P, E], U32, name="s_codes", align_bytes=64)
+        s_scales = sb.tile([P, E], U8, name="s_scales", align_bytes=64)
+
+        def load_q(i):
+            nc.sync.dma_start(out=q_raw[i][:], in_=q_rows[:, :, i * PIECE : (i + 1) * PIECE])
+
+        def load_og(c, g):
+            nc.sync.dma_start(out=og_raw[c][g][:], in_=og_rows[c, :, 2 * g : 2 * g + 2, :])
+
+        def sigmoid_q(i):
+            for a in range(2):
+                nc.scalar.activation(
+                    out=q_sig[i][:, :, a, :, :],
+                    in_=q_raw[i][:, 2 * a : 2 * a + 2, :].rearrange("p b (m r) -> p m r b", r=DEAL),
+                    func=SIGMOID,
+                )
+
+        def sigmoid_og(c, h):
+            nc.scalar.activation(out=gate[c][h][:], in_=og_raw[c][h // 2][:, h % 2, :], func=SIGMOID)
+
+        def weigh(i, u):
+            c, half = divmod(i, 2)
+            nc.vector.tensor_tensor(
+                out=fq[c][u][:, :, half * PIECE_M : (half + 1) * PIECE_M, :].rearrange("p r m (a b) -> p r (m a) b", b=2),
+                in0=q_sig[i][:, :, :, 2 * u : 2 * u + 2, :].rearrange("p m a r b -> p r (m a) b"),
+                in1=qa_rep[:].rearrange("p m (a b) -> p (m a) b", b=2).unsqueeze(1).to_broadcast([P, 2, 2 * PIECE_M, 2]),
+                op=MULT,
+            )
+
+        def quantize_fq(c, u):
+            nc.vector.quantize_mx(
+                out=fq_codes[c][u][:].bitcast(FP8X4),
+                scales=fq_scales[c][u][:],
+                in_=fq[c][u][:].rearrange("p r m j -> p (r m j)"),
+            )
+
+        def multiply(c, u):
+            for r in range(2):
+                cols = slice(r * P, (r + 1) * P)
+                place = 2 * u + r
+                for h in range(H):
+                    rows = slice(h * ROWS, (h + 1) * ROWS)
+                    nc.tensor.matmul_mx(
+                        out=acc[c][h][:, place * E : (place + 1) * E],
+                        lhsT=fq_codes[c][u][rows, cols].bitcast(FP8X4),
+                        lhsT_scale=fq_scales[c][u][rows, cols],
+                        rhs=s_codes[rows, :].bitcast(FP8X4),
+                        rhs_scale=s_scales[rows, :],
+                        start=True,
+                        stop=True,
+                    )
+
+        def finish(c, h):
+            nc.vector.tensor_tensor(out=res[c][h][:], in0=acc[c][h][:], in1=gate[c][h][:], op=MULT)
+            nc.sync.dma_start(out=out_rows[c, :, h, :], in_=res[c][h][:])
+
+        nc.scalar.dma_start(out=qa_sb[:], in_=qa.rearrange("(p j) o -> p (j o)", j=PACK).partition_broadcast(H))
+        load_q(0)
+        load_q(1)
+        nc.sync.dma_start(out=s_raw[:], in_=s_rows)
+        load_q(2)
+        load_og(0, 0)
+        load_q(3)
+        load_og(0, 1)
+        load_og(1, 0)
+        load_og(1, 1)
+
+        nc.vector.tensor_copy(out=qa_rep[:], in_=qa_sb[:].unsqueeze(1).to_broadcast([P, PIECE_M, PACK]))
+
+        sigmoid_q(0)
+        weigh(0, 0)
+        weigh(0, 1)
+        sigmoid_q(1)
+        nc.scalar.copy(out=s_bf[:], in_=s_raw[:].rearrange("p j e -> p e j"))
+        weigh(1, 0)
+        weigh(1, 1)
+        quantize_fq(0, 0)
+        nc.vector.quantize_mx(
+            out=s_codes[:].bitcast(FP8X4), scales=s_scales[:], in_=s_bf[:].rearrange("p e j -> p (e j)")
+        )
+        quantize_fq(0, 1)
+        multiply(0, 0)
+        multiply(0, 1)
+        sigmoid_q(2)
+        weigh(2, 0)
+        weigh(2, 1)
+        sigmoid_og(0, 0)
+        sigmoid_og(0, 1)
+        finish(0, 0)
+        finish(0, 1)
+        sigmoid_q(3)
+        weigh(3, 0)
+        weigh(3, 1)
+        quantize_fq(1, 0)
+        quantize_fq(1, 1)
+        multiply(1, 0)
+        multiply(1, 1)
+        for h in (2, 3):
+            sigmoid_og(0, h)
+            finish(0, h)
+        for h in range(H):
+            sigmoid_og(1, h)
+            finish(1, h)

@@ -19,7 +19,8 @@ PACK = 4
 CHUNK = 512
 DEAL = CHUNK // P
 PIECE = 256
-PIECE_M = PIECE // DEAL
+STEP = 128
+STEP_M = STEP // DEAL
 
 
 def tile_rows_read_sig_gate_kernel(tc, q, qa, S, og, out):
@@ -35,8 +36,8 @@ def tile_rows_read_sig_gate_kernel(tc, q, qa, S, og, out):
         ctx.enter_context(tc.manual_schedule())
 
         q_raw = [sb.tile([P, PACK, PIECE], F32, name="q_raw%d" % i) for i in range(4)]
-        q_sig = [sb.tile([P, PIECE_M, 2, DEAL, 2], F32, name="q_sig%d" % i) for i in range(4)]
-        fq = [[sb.tile([P, 2, P, PACK], BF16, name="fq%d_%d" % (c, u), align_bytes=64) for u in range(2)] for c in range(2)]
+        q_sig = [sb.tile([P, STEP_M, 2, DEAL, 2], F32, name="q_sig%d" % i) for i in range(8)]
+        fq = [sb.tile([P, DEAL, P, PACK], BF16, name="fq%d" % c, align_bytes=64) for c in range(2)]
         fq_codes = [[sb.tile([P, 2 * P], U32, name="fqc%d_%d" % (c, u), align_bytes=64) for u in range(2)] for c in range(2)]
         fq_scales = [[sb.tile([P, 2 * P], U8, name="fqs%d_%d" % (c, u), align_bytes=64) for u in range(2)] for c in range(2)]
         og_raw = [[sb.tile([P, 2, CHUNK], F32, name="og_raw%d_%d" % (c, g)) for g in range(2)] for c in range(2)]
@@ -44,7 +45,7 @@ def tile_rows_read_sig_gate_kernel(tc, q, qa, S, og, out):
         res = [[sb.tile([P, CHUNK], F32, name="res%d_%d" % (c, h)) for h in range(H)] for c in range(2)]
         acc = [[ps.tile([P, CHUNK], F32, name="acc%d_%d" % (c, h)) for h in range(H)] for c in range(2)]
         qa_sb = sb.tile([P, PACK], F32, name="qa_sb")
-        qa_rep = sb.tile([P, PIECE_M, PACK], F32, name="qa_rep")
+        qa_rep = sb.tile([P, STEP_M, PACK], F32, name="qa_rep")
         s_raw = sb.tile([P, PACK, E], F32, name="s_raw")
         s_bf = sb.tile([P, E, PACK], BF16, name="s_bf", align_bytes=64)
         s_codes = sb.tile([P, E], U32, name="s_codes", align_bytes=64)
@@ -56,50 +57,50 @@ def tile_rows_read_sig_gate_kernel(tc, q, qa, S, og, out):
         def load_og(c, g):
             nc.sync.dma_start(out=og_raw[c][g][:], in_=og_rows[c, :, 2 * g : 2 * g + 2, :])
 
-        def sigmoid_q(i):
+        def map_queries(s):
+            i, part = divmod(s, PIECE // STEP)
+            c, place = divmod(s, CHUNK // STEP)
             for a in range(2):
                 nc.scalar.activation(
-                    out=q_sig[i][:, :, a, :, :],
-                    in_=q_raw[i][:, 2 * a : 2 * a + 2, :].rearrange("p b (m r) -> p m r b", r=DEAL),
+                    out=q_sig[s][:, :, a, :, :],
+                    in_=q_raw[i][:, 2 * a : 2 * a + 2, part * STEP : (part + 1) * STEP].rearrange("p b (m r) -> p m r b", r=DEAL),
                     func=SIGMOID,
                 )
+            nc.vector.tensor_tensor(
+                out=fq[c][:, :, place * STEP_M : (place + 1) * STEP_M, :].rearrange("p r m (a b) -> p r (m a) b", b=2),
+                in0=q_sig[s][:].rearrange("p m a r b -> p r (m a) b"),
+                in1=qa_rep[:].rearrange("p m (a b) -> p (m a) b", b=2).unsqueeze(1).to_broadcast([P, DEAL, 2 * STEP_M, 2]),
+                op=MULT,
+            )
 
         def sigmoid_og(c, h):
             nc.scalar.activation(out=gate[c][h][:], in_=og_raw[c][h // 2][:, h % 2, :], func=SIGMOID)
 
-        def weigh(i, u):
-            c, half = divmod(i, 2)
-            nc.vector.tensor_tensor(
-                out=fq[c][u][:, :, half * PIECE_M : (half + 1) * PIECE_M, :].rearrange("p r m (a b) -> p r (m a) b", b=2),
-                in0=q_sig[i][:, :, :, 2 * u : 2 * u + 2, :].rearrange("p m a r b -> p r (m a) b"),
-                in1=qa_rep[:].rearrange("p m (a b) -> p (m a) b", b=2).unsqueeze(1).to_broadcast([P, 2, 2 * PIECE_M, 2]),
-                op=MULT,
-            )
-
-        def quantize_fq(c, u):
-            nc.vector.quantize_mx(
-                out=fq_codes[c][u][:].bitcast(FP8X4),
-                scales=fq_scales[c][u][:],
-                in_=fq[c][u][:].rearrange("p r m j -> p (r m j)"),
-            )
-
-        def multiply(c, u):
-            for r in range(2):
-                cols = slice(r * P, (r + 1) * P)
-                place = 2 * u + r
-                for h in range(H):
-                    rows = slice(h * ROWS, (h + 1) * ROWS)
-                    nc.tensor.matmul_mx(
-                        out=acc[c][h][:, place * E : (place + 1) * E],
-                        lhsT=fq_codes[c][u][rows, cols].bitcast(FP8X4),
-                        lhsT_scale=fq_scales[c][u][rows, cols],
-                        rhs=s_codes[rows, :].bitcast(FP8X4),
-                        rhs_scale=s_scales[rows, :],
-                        start=True,
-                        stop=True,
-                    )
+        def quantize_and_multiply(c):
+            for u in range(2):
+                nc.vector.quantize_mx(
+                    out=fq_codes[c][u][:].bitcast(FP8X4),
+                    scales=fq_scales[c][u][:],
+                    in_=fq[c][:, 2 * u : 2 * u + 2, :, :].rearrange("p r m j -> p (r m j)"),
+                )
+            for first in range(0, H, 2):
+                for r in range(DEAL):
+                    u = r // 2
+                    cols = slice((r % 2) * P, (r % 2 + 1) * P)
+                    for h in (first, first + 1):
+                        rows = slice(h * ROWS, (h + 1) * ROWS)
+                        nc.tensor.matmul_mx(
+                            out=acc[c][h][:, r * E : (r + 1) * E],
+                            lhsT=fq_codes[c][u][rows, cols].bitcast(FP8X4),
+                            lhsT_scale=fq_scales[c][u][rows, cols],
+                            rhs=s_codes[rows, :].bitcast(FP8X4),
+                            rhs_scale=s_scales[rows, :],
+                            start=True,
+                            stop=True,
+                        )
 
         def finish(c, h):
+            sigmoid_og(c, h)
             nc.vector.tensor_tensor(out=res[c][h][:], in0=acc[c][h][:], in1=gate[c][h][:], op=MULT)
             nc.sync.dma_start(out=out_rows[c, :, h, :], in_=res[c][h][:])
 
@@ -108,45 +109,26 @@ def tile_rows_read_sig_gate_kernel(tc, q, qa, S, og, out):
         load_q(1)
         nc.sync.dma_start(out=s_raw[:], in_=s_rows)
         load_q(2)
-        load_og(0, 0)
         load_q(3)
+        load_og(0, 0)
         load_og(0, 1)
         load_og(1, 0)
         load_og(1, 1)
 
-        nc.vector.tensor_copy(out=qa_rep[:], in_=qa_sb[:].unsqueeze(1).to_broadcast([P, PIECE_M, PACK]))
+        nc.vector.tensor_copy(out=qa_rep[:], in_=qa_sb[:].unsqueeze(1).to_broadcast([P, STEP_M, PACK]))
 
-        sigmoid_q(0)
-        weigh(0, 0)
-        weigh(0, 1)
-        sigmoid_q(1)
+        for s in range(4):
+            map_queries(s)
         nc.scalar.copy(out=s_bf[:], in_=s_raw[:].rearrange("p j e -> p e j"))
-        weigh(1, 0)
-        weigh(1, 1)
-        quantize_fq(0, 0)
         nc.vector.quantize_mx(
             out=s_codes[:].bitcast(FP8X4), scales=s_scales[:], in_=s_bf[:].rearrange("p e j -> p (e j)")
         )
-        quantize_fq(0, 1)
-        multiply(0, 0)
-        multiply(0, 1)
-        sigmoid_q(2)
-        weigh(2, 0)
-        weigh(2, 1)
-        sigmoid_og(0, 0)
-        sigmoid_og(0, 1)
+        quantize_and_multiply(0)
+        for s in range(4, 8):
+            map_queries(s)
         finish(0, 0)
-        finish(0, 1)
-        sigmoid_q(3)
-        weigh(3, 0)
-        weigh(3, 1)
-        quantize_fq(1, 0)
-        quantize_fq(1, 1)
-        multiply(1, 0)
-        multiply(1, 1)
-        for h in (2, 3):
-            sigmoid_og(0, h)
+        quantize_and_multiply(1)
+        for h in range(1, H):
             finish(0, h)
         for h in range(H):
-            sigmoid_og(1, h)
             finish(1, h)

from contextlib import ExitStack

import concourse.mybir as mybir

H, D, N, E = 4, 128, 1024, 128
FLOPS = 2 * H * N * D * E

F32 = mybir.dt.float32
BF16 = mybir.dt.bfloat16
U32 = mybir.dt.uint32
U8 = mybir.dt.uint8
FP8X4 = mybir.dt.float8_e4m3fn_x4
SIGMOID = mybir.ActivationFunctionType.Sigmoid
MULT = mybir.AluOpType.mult

P = 128
ROWS = 32
PACK = 4
CHUNK = 512
DEAL = CHUNK // P
PIECE = 256
STEP = 128
STEP_M = STEP // DEAL


def tile_rows_read_sig_gate_kernel(tc, q, qa, S, og, out):
    nc = tc.nc
    q_rows = q.rearrange("h (p j) n -> (h p) j n", j=PACK)
    s_rows = S.rearrange("h (p j) e -> (h p) j e", j=PACK)
    og_rows = og.rearrange("h (c m r) e -> c m h (r e)", m=P, r=DEAL)
    out_rows = out.rearrange("h (c m r) e -> c m h (r e)", m=P, r=DEAL)

    with ExitStack() as ctx:
        sb = ctx.enter_context(tc.tile_pool(name="sb", bufs=1))
        ps = ctx.enter_context(tc.psum_pool(name="ps", bufs=1))
        ctx.enter_context(tc.manual_schedule())

        q_raw = [sb.tile([P, PACK, PIECE], F32, name="q_raw%d" % i) for i in range(4)]
        q_sig = [sb.tile([P, STEP_M, 2, DEAL, 2], F32, name="q_sig%d" % i) for i in range(8)]
        fq = [sb.tile([P, DEAL, P, PACK], BF16, name="fq%d" % c, align_bytes=64) for c in range(2)]
        fq_codes = [[sb.tile([P, 2 * P], U32, name="fqc%d_%d" % (c, u), align_bytes=64) for u in range(2)] for c in range(2)]
        fq_scales = [[sb.tile([P, 2 * P], U8, name="fqs%d_%d" % (c, u), align_bytes=64) for u in range(2)] for c in range(2)]
        og_raw = [[sb.tile([P, 2, CHUNK], F32, name="og_raw%d_%d" % (c, g)) for g in range(2)] for c in range(2)]
        gate = [[sb.tile([P, CHUNK], F32, name="gate%d_%d" % (c, h)) for h in range(H)] for c in range(2)]
        res = [[sb.tile([P, CHUNK], F32, name="res%d_%d" % (c, h)) for h in range(H)] for c in range(2)]
        acc = [[ps.tile([P, CHUNK], F32, name="acc%d_%d" % (c, h)) for h in range(H)] for c in range(2)]
        qa_sb = sb.tile([P, PACK], F32, name="qa_sb")
        qa_rep = sb.tile([P, STEP_M, PACK], F32, name="qa_rep")
        s_raw = sb.tile([P, PACK, E], F32, name="s_raw")
        s_bf = sb.tile([P, E, PACK], BF16, name="s_bf", align_bytes=64)
        s_codes = sb.tile([P, E], U32, name="s_codes", align_bytes=64)
        s_scales = sb.tile([P, E], U8, name="s_scales", align_bytes=64)

        def load_q(i):
            nc.sync.dma_start(out=q_raw[i][:], in_=q_rows[:, :, i * PIECE : (i + 1) * PIECE])

        def load_og(c, g):
            nc.sync.dma_start(out=og_raw[c][g][:], in_=og_rows[c, :, 2 * g : 2 * g + 2, :])

        def map_queries(s):
            i, part = divmod(s, PIECE // STEP)
            c, place = divmod(s, CHUNK // STEP)
            for a in range(2):
                nc.scalar.activation(
                    out=q_sig[s][:, :, a, :, :],
                    in_=q_raw[i][:, 2 * a : 2 * a + 2, part * STEP : (part + 1) * STEP].rearrange("p b (m r) -> p m r b", r=DEAL),
                    func=SIGMOID,
                )
            nc.vector.tensor_tensor(
                out=fq[c][:, :, place * STEP_M : (place + 1) * STEP_M, :].rearrange("p r m (a b) -> p r (m a) b", b=2),
                in0=q_sig[s][:].rearrange("p m a r b -> p r (m a) b"),
                in1=qa_rep[:].rearrange("p m (a b) -> p (m a) b", b=2).unsqueeze(1).to_broadcast([P, DEAL, 2 * STEP_M, 2]),
                op=MULT,
            )

        def sigmoid_og(c, h):
            nc.scalar.activation(out=gate[c][h][:], in_=og_raw[c][h // 2][:, h % 2, :], func=SIGMOID)

        def quantize_and_multiply(c):
            for u in range(2):
                nc.vector.quantize_mx(
                    out=fq_codes[c][u][:].bitcast(FP8X4),
                    scales=fq_scales[c][u][:],
                    in_=fq[c][:, 2 * u : 2 * u + 2, :, :].rearrange("p r m j -> p (r m j)"),
                )
            for first in range(0, H, 2):
                for r in range(DEAL):
                    u = r // 2
                    cols = slice((r % 2) * P, (r % 2 + 1) * P)
                    for h in (first, first + 1):
                        rows = slice(h * ROWS, (h + 1) * ROWS)
                        nc.tensor.matmul_mx(
                            out=acc[c][h][:, r * E : (r + 1) * E],
                            lhsT=fq_codes[c][u][rows, cols].bitcast(FP8X4),
                            lhsT_scale=fq_scales[c][u][rows, cols],
                            rhs=s_codes[rows, :].bitcast(FP8X4),
                            rhs_scale=s_scales[rows, :],
                            start=True,
                            stop=True,
                        )

        def finish(c, h):
            sigmoid_og(c, h)
            nc.vector.tensor_tensor(out=res[c][h][:], in0=acc[c][h][:], in1=gate[c][h][:], op=MULT)
            nc.sync.dma_start(out=out_rows[c, :, h, :], in_=res[c][h][:])

        nc.scalar.dma_start(out=qa_sb[:], in_=qa.rearrange("(p j) o -> p (j o)", j=PACK).partition_broadcast(H))
        load_q(0)
        load_q(1)
        nc.sync.dma_start(out=s_raw[:], in_=s_rows)
        load_q(2)
        load_q(3)
        load_og(0, 0)
        load_og(0, 1)
        load_og(1, 0)
        load_og(1, 1)

        nc.vector.tensor_copy(out=qa_rep[:], in_=qa_sb[:].unsqueeze(1).to_broadcast([P, STEP_M, PACK]))

        for s in range(4):
            map_queries(s)
        nc.scalar.copy(out=s_bf[:], in_=s_raw[:].rearrange("p j e -> p e j"))
        nc.vector.quantize_mx(
            out=s_codes[:].bitcast(FP8X4), scales=s_scales[:], in_=s_bf[:].rearrange("p e j -> p (e j)")
        )
        quantize_and_multiply(0)
        for s in range(4, 8):
            map_queries(s)
        finish(0, 0)
        quantize_and_multiply(1)
        for h in range(1, H):
            finish(0, h)
        for h in range(H):
            finish(1, h)
